import numpy as np
CORES = [34,162,290,418,42,426]
N = 6
F = 32
BOUND = 4063.9
def setup_inputs(rng):
    gr = rng.standard_normal((1, 128, N * F), dtype=np.float32) + rng.standard_normal((N, 128, N * F), dtype=np.float32)
    return {"gr": gr}
def setup_inputs_big(rng):
    d = setup_inputs(rng)
    for k in ("gr",): d[k] = (d[k].astype(np.float32) * 1024.0).astype(d[k].dtype)
    return d
def setup_inputs_small(rng):
    d = setup_inputs(rng)
    for k in ("gr",): d[k] = (d[k].astype(np.float32) * (1 / 1024.0)).astype(d[k].dtype)
    return d
def setup_inputs_apart(rng):
    d = setup_inputs(rng)
    f = (10.0 ** rng.permutation(np.linspace(-1.5, 1.5, N))).astype(np.float32).reshape(N, 1, 1)
    for k in ("gr",): d[k] = (d[k].astype(np.float32) * f).astype(d[k].dtype)
    return d
def setup_inputs_far(rng):
    d = setup_inputs(rng)
    for k in ("gr",): d[k] = (d[k].astype(np.float32) * 16384.0).astype(d[k].dtype)
    return d
def setup_inputs_over(rng):
    d = setup_inputs(rng)
    f = np.float32(10.0 ** rng.uniform(1.5, 3.5)) * np.where(rng.random((1, 128, N * F)) < 0.5, 0.1, 1.0).astype(np.float32)
    for k in ("gr",): d[k] = (d[k].astype(np.float32) * f).astype(d[k].dtype)
    return d
def reference(gr):
    s = gr.astype(np.float64).sum(axis=0)
    nrm = np.sqrt((s ** 2).sum())
    s = s * min(1.0, BOUND / nrm)
    return {"y": np.stack([s[:, F * r:F * r + F] for r in range(N)]).astype(np.float32)}

@@ -1,0 +1,225 @@
+import math
+from concourse.bass import DstId, RemoteDMATransfer
+from concourse.mybir import AluOpType, ActivationFunctionType
+
+N, F = 6, 32
+W = N * F
+K = 128
+RHO = 2.0 ** 0.9
+SIG = 2.0 ** -8
+TAU0 = SIG * SIG
+TAUL = TAU0 * RHO ** (K - 1)
+
+
+def _dip():
+    w = 1.0
+    for i in range(2001):
+        e = 1.0 + (RHO - 1.0) * i / 2000.0
+        w = min(w, max(1.5 - 0.5 * e, (1.5 - 0.5 * e / RHO) / math.sqrt(RHO)) * math.sqrt(e))
+    return 1.0 - w
+
+
+LAM = (SIG / 16.0) ** (1.0 / 9.0)
+GLAST = 0.5 * LAM / (1.0 - 0.5 * _dip()) / math.sqrt(TAUL)
+NEWTON1 = 3.0 * LAM ** 2
+NEWTON2 = 12.0 * LAM ** 6
+
+SCRATCH = {
+    "gd": ("dram", [128, W], "float32"),
+    "rl": ("dram", [2, 128, W], "float32"),
+    "yl": ("dram", [128, F], "float32"),
+    "own": ("sbuf", [128, W], "float32"),
+    "l2": ("sbuf", [128, W], "float32"),
+    "l3": ("sbuf", [128, W], "float32"),
+    "s": ("sbuf", [128, W], "float32"),
+    "ones": ("sbuf", [128, 128], "float32"),
+    "geo": ("sbuf", [128, K], "float32"),
+    "ntau": ("sbuf", [128, K], "float32"),
+    "rt": ("sbuf", [128, K], "float32"),
+    "env": ("sbuf", [128, K], "float32"),
+    "col": ("sbuf", [128, 8], "float32"),
+    "acc": ("psum", [128, W], "float32"),
+    "tp": ("psum", [128, 1], "float32"),
+}
+SEMAPHORES = ["ld", "ldo", "sent", "r1", "a2", "a3", "ms", "tb", "ch", "yr", "yo", "fin", "st"]
+
+_PLAN = {}
+
+
+def _steps(topo, a, b):
+    if topo.rack(topo.host(a)) == topo.rack(topo.host(b)):
+        return 1 if (topo.mates(a, b) or topo.same_plane(a, b)) else 2
+    return 1 if topo.chip(a) == topo.chip(b) else 3
+
+
+def _pairs(xs):
+    return [(xs[i], xs[j]) for i in range(len(xs)) for j in range(i + 1, len(xs))]
+
+
+def _tree(topo, hub, rel, kids):
+    best = None
+    for code in range(2 ** len(kids)):
+        par = [rel[(code >> i) & 1] for i in range(len(kids))]
+        if not all(topo.may_write(k, p) for k, p in zip(kids, par)):
+            continue
+        if any(r not in par for r in rel):
+            continue
+        tot = sum(_steps(topo, k, p) for k, p in zip(kids, par)) + sum(_steps(topo, r, hub) for r in rel)
+        worst = max(sum(_steps(topo, k, p) for k, p in zip(kids, par) if p == r) for r in rel)
+        if best is None or (tot, worst) < best[0]:
+            best = ((tot, worst), dict(zip(kids, par)))
+    return best
+
+
+def make_plan(cores, topo):
+    best = None
+    for u, v in _pairs(list(cores)):
+        if topo.may_write(u, v) or topo.may_write(v, u):
+            continue
+        rest = [c for c in cores if c != u and c != v]
+        for ru in _pairs(rest):
+            rv = tuple(c for c in rest if c not in ru)
+            if not (all(topo.may_write(r, u) for r in ru) and all(topo.may_write(r, v) for r in rv)):
+                continue
+            tu = _tree(topo, u, ru, (v,) + rv)
+            tv = _tree(topo, v, rv, (u,) + ru)
+            if tu is None or tv is None:
+                continue
+            for cu in _pairs(rest):
+                cv = tuple(c for c in rest if c not in cu)
+                if not (all(topo.may_write(u, c) for c in cu) and all(topo.may_write(v, c) for c in cv)):
+                    continue
+                cost = (tu[0][0] + tv[0][0] + sum(_steps(topo, u, c) for c in cu) + sum(_steps(topo, v, c) for c in cv),
+                        max(tu[0][1], tv[0][1]))
+                if best is None or cost < best[0]:
+                    best = (cost, {u: (ru, tu[1], cu), v: (rv, tv[1], cv)})
+    return best[1]
+
+
+def _count(mask):
+    return bin(mask).count("1")
+
+
+def _halves(mask):
+    bits = [1 << i for i in range(mask.bit_length()) if (mask >> i) & 1]
+    h = len(bits) // 2
+    return sum(bits[:h]), sum(bits[h:])
+
+
+def rank_program(g, core, T, topo):
+    rank = T.rank_of(core)
+    if rank is None:
+        return
+    if "p" not in _PLAN:
+        _PLAN["p"] = make_plan(list(T.cores), topo)
+    plan = _PLAN["p"]
+    sem = T.sem
+    mult, add, amax, amin, sub = AluOpType.mult, AluOpType.add, AluOpType.max, AluOpType.min, AluOpType.subtract
+    Q, V, S, P = g.sync, g.vector, g.scalar, g.tensor
+    is_hub = core in plan
+
+    Q.dma_start(T.gd[:], T.gr[:]).then_inc(sem.ld, 16)
+    if is_hub:
+        Q.dma_start(T.own[:], T.gr[:]).then_inc(sem.ldo, 16)
+
+    parent, slot = None, None
+    for hub in plan:
+        send = plan[hub][1]
+        if core in send:
+            parent = send[core]
+            slot = [k for k in send if send[k] == parent].index(core)
+    sent = 0
+    m = topo.mask(core, parent)
+    rid, pid = topo.addr(parent, core)
+    g.wait_ge(sem.ld, 16)
+    g.remote_dma(out_ap=T.rl[slot], in_ap=T.gd[:], remote_sem=sem.r1, local_sem=sem.sent, pid=pid, routing_id=rid,
+                 dma_engine_mask=m)
+    sent += _count(m)
+
+    if not is_hub:
+        hub = [h for h in plan if core in plan[h][0]][0]
+        kids = [k for k in plan[hub][1] if plan[hub][1][k] == core]
+        first = plan[hub][0].index(core) == 0
+        m = topo.mask(core, hub)
+        rid, pid = topo.addr(hub, core)
+        g.wait_ge(sem.r1, sum(_count(topo.mask(k, core)) for k in kids))
+        g.remote_dma_fused([RemoteDMATransfer(
+            dst_ids=[DstId(rid=rid, pnc=pid)], dma_engine_mask=m, remote_sem=sem.a2 if first else sem.a3,
+            srcs=[T.gd[:]] + [T.rl[i] for i in range(len(kids))], dsts=[T.l2[:] if first else T.l3[:]], alu_op=1)],
+            local_sem=sem.sent)
+        sent += _count(m)
+        g.wait_ge(sem.sent, sent)
+        server = [h for h in plan if core in plan[h][2]][0]
+        both = topo.mask(server, plan[server][2][0]) & topo.mask(server, plan[server][2][1])
+        Q.wait_ge(sem.fin, _count(_halves(both)[plan[server][2].index(core)]))
+        Q.dma_start(T.y[:], T.yl[:]).then_inc(sem.st, 16)
+        Q.wait_ge(sem.st, 16)
+        return
+
+    relays, _, clients = plan[core]
+    col = T.col
+    q, t, a0, y1, a1, c = (col[:, i:i + 1] for i in range(6))
+    y0 = T.env[:, K - 1:K]
+
+    def blk(cr):
+        r = T.rank_of(cr)
+        return T.s[:, r * F:(r + 1) * F]
+
+    V.memset(T.ones[:], 1.0).then_inc(sem.ms, 1)
+    V.memset(T.geo[:], 1.0 / RHO).then_inc(sem.ms, 1)
+    V.memset(T.rt[:, 0:K - 1], math.sqrt(RHO)).then_inc(sem.ms, 1)
+    V.memset(T.rt[:, K - 1:K], GLAST).then_inc(sem.ms, 1)
+    V.wait_ge(sem.ms, 4)
+    V.tensor_tensor_scan(T.ntau[:], T.geo[:], T.ones[:, 0:K], -RHO / TAU0, mult, mult).then_inc(sem.tb, 1)
+
+    V.wait_ge(sem.ldo, 16)
+    V.tensor_copy(T.acc[:], T.own[:]).then_inc(sem.ch, 1)
+    V.wait_ge(sem.a2, _count(topo.mask(relays[0], core)))
+    V.wait_ge(sem.ch, 1)
+    V.tensor_tensor(T.acc[:], T.acc[:], T.l2[:], add).then_inc(sem.ch, 1)
+    V.wait_ge(sem.a3, _count(topo.mask(relays[1], core)))
+    V.wait_ge(sem.ch, 2)
+    V.tensor_tensor(T.s[:], T.acc[:], T.l3[:], add).then_inc(sem.ch, 1)
+
+    S.wait_ge(sem.ch, 3)
+    S.activation(T.own[:], T.s[:], ActivationFunctionType.Square, scale=SIG / float(T.tables["BOUND"]),
+                 accum_out=q).then_inc(sem.ch, 1)
+    P.wait_ge(sem.ms, 4)
+    P.wait_ge(sem.ch, 4)
+    P.matmul(T.tp[:], T.ones[:], q, True, True).then_inc(sem.ch, 1)
+
+    V.wait_ge(sem.tb, 1)
+    V.wait_ge(sem.ch, 5)
+    V.tensor_scalar(t, T.tp[:], TAU0, TAUL, amax, amin).then_inc(sem.ch, 1)
+    V.wait_ge(sem.ch, 6)
+    V.tensor_scalar(T.geo[:], T.ntau[:], t, 3.0, mult, add).then_inc(sem.ch, 1)
+    V.wait_ge(sem.ch, 7)
+    V.tensor_tensor_scan(T.env[:], T.geo[:], T.rt[:], -1.0e29, amax, mult).then_inc(sem.ch, 1)
+    V.wait_ge(sem.ch, 8)
+    V.tensor_scalar(a0, y0, y0, t, mult, mult).then_inc(sem.ch, 1)
+    V.wait_ge(sem.ch, 9)
+    V.tensor_scalar(y1, a0, NEWTON1, y0, sub, mult).then_inc(sem.ch, 1)
+    V.wait_ge(sem.ch, 10)
+    V.tensor_scalar(a1, y1, y1, t, mult, mult).then_inc(sem.ch, 1)
+    V.wait_ge(sem.ch, 11)
+    V.tensor_scalar(c, a1, NEWTON2, y1, sub, mult).then_inc(sem.ch, 1)
+
+    V.wait_ge(sem.ch, 12)
+    V.tensor_scalar(blk(clients[0]), blk(clients[0]), c, None, mult).then_inc(sem.yr, 1)
+    S.wait_ge(sem.ch, 12)
+    S.activation(blk(clients[1]), blk(clients[1]), ActivationFunctionType.Copy, scale=c).then_inc(sem.yr, 1)
+    V.tensor_scalar(blk(core), blk(core), c, None, mult).then_inc(sem.yo, 1)
+
+    both = topo.mask(core, clients[0]) & topo.mask(core, clients[1])
+    trs = []
+    for cl, m in zip(clients, _halves(both)):
+        rid, pid = topo.addr(cl, core)
+        trs.append(RemoteDMATransfer(dst_ids=[DstId(rid=rid, pnc=pid)], dma_engine_mask=m, remote_sem=sem.fin,
+                                     src=blk(cl), dst=T.yl[:]))
+        sent += _count(m)
+    g.wait_ge(sem.yr, 2)
+    g.remote_dma_fused(trs, local_sem=sem.sent)
+    Q.wait_ge(sem.yo, 1)
+    Q.dma_start(T.y[:], blk(core)).then_inc(sem.st, 16)
+    Q.wait_ge(sem.st, 16)
+    g.wait_ge(sem.sent, sent)

@@ -26,11 +26,10 @@ NEWTON2 = 12.0 * LAM ** 6
 
 SCRATCH = {
     "gd": ("dram", [128, W], "float32"),
-    "rl": ("dram", [2, 128, W], "float32"),
-    "yl": ("dram", [128, F], "float32"),
     "own": ("sbuf", [128, W], "float32"),
+    "l0": ("sbuf", [128, W], "float32"),
+    "l1": ("sbuf", [128, W], "float32"),
     "l2": ("sbuf", [128, W], "float32"),
-    "l3": ("sbuf", [128, W], "float32"),
     "s": ("sbuf", [128, W], "float32"),
     "ones": ("sbuf", [128, 128], "float32"),
     "geo": ("sbuf", [128, K], "float32"),
@@ -41,59 +40,16 @@ SCRATCH = {
     "acc": ("psum", [128, W], "float32"),
     "tp": ("psum", [128, 1], "float32"),
 }
-SEMAPHORES = ["ld", "ldo", "sent", "r1", "a2", "a3", "ms", "tb", "ch", "yr", "yo", "fin", "st"]
-
-_PLAN = {}
+SEMAPHORES = ["ld", "ldo", "sent", "r1", "a3", "ms", "tb", "ch", "yo", "st"]
 
 
-def _steps(topo, a, b):
-    if topo.rack(topo.host(a)) == topo.rack(topo.host(b)):
-        return 1 if (topo.mates(a, b) or topo.same_plane(a, b)) else 2
-    return 1 if topo.chip(a) == topo.chip(b) else 3
+def _peers(cores, topo, c):
+    return [x for x in cores if x != c and topo.rack(topo.host(x)) == topo.rack(topo.host(c))]
 
 
-def _pairs(xs):
-    return [(xs[i], xs[j]) for i in range(len(xs)) for j in range(i + 1, len(xs))]
-
-
-def _tree(topo, hub, rel, kids):
-    best = None
-    for code in range(2 ** len(kids)):
-        par = [rel[(code >> i) & 1] for i in range(len(kids))]
-        if not all(topo.may_write(k, p) for k, p in zip(kids, par)):
-            continue
-        if any(r not in par for r in rel):
-            continue
-        tot = sum(_steps(topo, k, p) for k, p in zip(kids, par)) + sum(_steps(topo, r, hub) for r in rel)
-        worst = max(sum(_steps(topo, k, p) for k, p in zip(kids, par) if p == r) for r in rel)
-        if best is None or (tot, worst) < best[0]:
-            best = ((tot, worst), dict(zip(kids, par)))
-    return best
-
-
-def make_plan(cores, topo):
-    best = None
-    for u, v in _pairs(list(cores)):
-        if topo.may_write(u, v) or topo.may_write(v, u):
-            continue
-        rest = [c for c in cores if c != u and c != v]
-        for ru in _pairs(rest):
-            rv = tuple(c for c in rest if c not in ru)
-            if not (all(topo.may_write(r, u) for r in ru) and all(topo.may_write(r, v) for r in rv)):
-                continue
-            tu = _tree(topo, u, ru, (v,) + rv)
-            tv = _tree(topo, v, rv, (u,) + ru)
-            if tu is None or tv is None:
-                continue
-            for cu in _pairs(rest):
-                cv = tuple(c for c in rest if c not in cu)
-                if not (all(topo.may_write(u, c) for c in cu) and all(topo.may_write(v, c) for c in cv)):
-                    continue
-                cost = (tu[0][0] + tv[0][0] + sum(_steps(topo, u, c) for c in cu) + sum(_steps(topo, v, c) for c in cv),
-                        max(tu[0][1], tv[0][1]))
-                if best is None or cost < best[0]:
-                    best = (cost, {u: (ru, tu[1], cu), v: (rv, tv[1], cv)})
-    return best[1]
+def _partner(cores, topo, c):
+    return [x for x in cores if topo.rack(topo.host(x)) != topo.rack(topo.host(c)) and topo.may_write(c, x)
+            and topo.chip(x) == topo.chip(c)][0]
 
 
 def _count(mask):
@@ -106,64 +62,50 @@ def _halves(mask):
     return sum(bits[:h]), sum(bits[h:])
 
 
+def _hop1_masks(cores, topo, c):
+    peers = _peers(cores, topo, c)
+    return dict(zip(peers, _halves(topo.mask(c, peers[0]) & topo.mask(c, peers[1]))))
+
+
 def rank_program(g, core, T, topo):
     rank = T.rank_of(core)
     if rank is None:
         return
-    if "p" not in _PLAN:
-        _PLAN["p"] = make_plan(list(T.cores), topo)
-    plan = _PLAN["p"]
+    cores = list(T.cores)
     sem = T.sem
     mult, add, amax, amin, sub = AluOpType.mult, AluOpType.add, AluOpType.max, AluOpType.min, AluOpType.subtract
     Q, V, S, P = g.sync, g.vector, g.scalar, g.tensor
-    is_hub = core in plan
+    peers = _peers(cores, topo, core)
+    partner = _partner(cores, topo, core)
+    land = [T.l0, T.l1]
 
     Q.dma_start(T.gd[:], T.gr[:]).then_inc(sem.ld, 16)
-    if is_hub:
-        Q.dma_start(T.own[:], T.gr[:]).then_inc(sem.ldo, 16)
+    Q.dma_start(T.own[:], T.gr[:]).then_inc(sem.ldo, 16)
 
-    parent, slot = None, None
-    for hub in plan:
-        send = plan[hub][1]
-        if core in send:
-            parent = send[core]
-            slot = [k for k in send if send[k] == parent].index(core)
     sent = 0
-    m = topo.mask(core, parent)
-    rid, pid = topo.addr(parent, core)
+    trs = []
+    masks = _hop1_masks(cores, topo, core)
+    for p in peers:
+        rid, pid = topo.addr(p, core)
+        trs.append(RemoteDMATransfer(dst_ids=[DstId(rid=rid, pnc=pid)], dma_engine_mask=masks[p], remote_sem=sem.r1,
+                                     src=T.gd[:], dst=land[_peers(cores, topo, p).index(core)][:]))
+        sent += _count(masks[p])
     g.wait_ge(sem.ld, 16)
-    g.remote_dma(out_ap=T.rl[slot], in_ap=T.gd[:], remote_sem=sem.r1, local_sem=sem.sent, pid=pid, routing_id=rid,
-                 dma_engine_mask=m)
+    g.remote_dma_fused(trs, local_sem=sem.sent)
+
+    landed = sum(_count(_hop1_masks(cores, topo, p)[core]) for p in peers)
+    m = topo.mask(core, partner)
+    rid, pid = topo.addr(partner, core)
+    g.wait_ge(sem.r1, landed)
+    g.remote_dma_fused([RemoteDMATransfer(dst_ids=[DstId(rid=rid, pnc=pid)], dma_engine_mask=m, remote_sem=sem.a3,
+                                          srcs=[T.gd[:], T.l0[:], T.l1[:]], dsts=[T.l2[:]], alu_op=1)],
+                       local_sem=sem.sent)
     sent += _count(m)
 
-    if not is_hub:
-        hub = [h for h in plan if core in plan[h][0]][0]
-        kids = [k for k in plan[hub][1] if plan[hub][1][k] == core]
-        first = plan[hub][0].index(core) == 0
-        m = topo.mask(core, hub)
-        rid, pid = topo.addr(hub, core)
-        g.wait_ge(sem.r1, sum(_count(topo.mask(k, core)) for k in kids))
-        g.remote_dma_fused([RemoteDMATransfer(
-            dst_ids=[DstId(rid=rid, pnc=pid)], dma_engine_mask=m, remote_sem=sem.a2 if first else sem.a3,
-            srcs=[T.gd[:]] + [T.rl[i] for i in range(len(kids))], dsts=[T.l2[:] if first else T.l3[:]], alu_op=1)],
-            local_sem=sem.sent)
-        sent += _count(m)
-        g.wait_ge(sem.sent, sent)
-        server = [h for h in plan if core in plan[h][2]][0]
-        both = topo.mask(server, plan[server][2][0]) & topo.mask(server, plan[server][2][1])
-        Q.wait_ge(sem.fin, _count(_halves(both)[plan[server][2].index(core)]))
-        Q.dma_start(T.y[:], T.yl[:]).then_inc(sem.st, 16)
-        Q.wait_ge(sem.st, 16)
-        return
-
-    relays, _, clients = plan[core]
     col = T.col
     q, t, a0, y1, a1, c = (col[:, i:i + 1] for i in range(6))
     y0 = T.env[:, K - 1:K]
-
-    def blk(cr):
-        r = T.rank_of(cr)
-        return T.s[:, r * F:(r + 1) * F]
+    mine = T.s[:, rank * F:(rank + 1) * F]
 
     V.memset(T.ones[:], 1.0).then_inc(sem.ms, 1)
     V.memset(T.geo[:], 1.0 / RHO).then_inc(sem.ms, 1)
@@ -173,13 +115,13 @@ def rank_program(g, core, T, topo):
     V.tensor_tensor_scan(T.ntau[:], T.geo[:], T.ones[:, 0:K], -RHO / TAU0, mult, mult).then_inc(sem.tb, 1)
 
     V.wait_ge(sem.ldo, 16)
-    V.tensor_copy(T.acc[:], T.own[:]).then_inc(sem.ch, 1)
-    V.wait_ge(sem.a2, _count(topo.mask(relays[0], core)))
+    V.wait_ge(sem.r1, landed)
+    V.tensor_tensor(T.acc[:], T.own[:], T.l0[:], add).then_inc(sem.ch, 1)
     V.wait_ge(sem.ch, 1)
-    V.tensor_tensor(T.acc[:], T.acc[:], T.l2[:], add).then_inc(sem.ch, 1)
-    V.wait_ge(sem.a3, _count(topo.mask(relays[1], core)))
+    V.tensor_tensor(T.acc[:], T.acc[:], T.l1[:], add).then_inc(sem.ch, 1)
+    V.wait_ge(sem.a3, _count(topo.mask(partner, core)))
     V.wait_ge(sem.ch, 2)
-    V.tensor_tensor(T.s[:], T.acc[:], T.l3[:], add).then_inc(sem.ch, 1)
+    V.tensor_tensor(T.s[:], T.acc[:], T.l2[:], add).then_inc(sem.ch, 1)
 
     S.wait_ge(sem.ch, 3)
     S.activation(T.own[:], T.s[:], ActivationFunctionType.Square, scale=SIG / float(T.tables["BOUND"]),
@@ -205,21 +147,8 @@ def rank_program(g, core, T, topo):
     V.tensor_scalar(c, a1, NEWTON2, y1, sub, mult).then_inc(sem.ch, 1)
 
     V.wait_ge(sem.ch, 12)
-    V.tensor_scalar(blk(clients[0]), blk(clients[0]), c, None, mult).then_inc(sem.yr, 1)
-    S.wait_ge(sem.ch, 12)
-    S.activation(blk(clients[1]), blk(clients[1]), ActivationFunctionType.Copy, scale=c).then_inc(sem.yr, 1)
-    V.tensor_scalar(blk(core), blk(core), c, None, mult).then_inc(sem.yo, 1)
-
-    both = topo.mask(core, clients[0]) & topo.mask(core, clients[1])
-    trs = []
-    for cl, m in zip(clients, _halves(both)):
-        rid, pid = topo.addr(cl, core)
-        trs.append(RemoteDMATransfer(dst_ids=[DstId(rid=rid, pnc=pid)], dma_engine_mask=m, remote_sem=sem.fin,
-                                     src=blk(cl), dst=T.yl[:]))
-        sent += _count(m)
-    g.wait_ge(sem.yr, 2)
-    g.remote_dma_fused(trs, local_sem=sem.sent)
+    V.tensor_scalar(mine, mine, c, None, mult).then_inc(sem.yo, 1)
     Q.wait_ge(sem.yo, 1)
-    Q.dma_start(T.y[:], blk(core)).then_inc(sem.st, 16)
+    Q.dma_start(T.y[:], mine).then_inc(sem.st, 16)
     Q.wait_ge(sem.st, 16)
     g.wait_ge(sem.sent, sent)

@@ -4,6 +4,7 @@ from concourse.mybir import AluOpType, ActivationFunctionType
 
 N, F = 6, 32
 W = N * F
+PW = 2 * F
 K = 128
 RHO = 2.0 ** 0.9
 SIG = 2.0 ** -8
@@ -25,22 +26,26 @@ NEWTON1 = 3.0 * LAM ** 2
 NEWTON2 = 12.0 * LAM ** 6
 
 SCRATCH = {
-    "gd": ("dram", [128, W], "float32"),
-    "own": ("sbuf", [128, W], "float32"),
-    "l0": ("sbuf", [128, W], "float32"),
-    "l1": ("sbuf", [128, W], "float32"),
-    "l2": ("sbuf", [128, W], "float32"),
-    "s": ("sbuf", [128, W], "float32"),
+    "gd": ("dram", [2, 128, PW], "float32"),
+    "in1": ("dram", [2, 128, PW], "float32"),
+    "ownp": ("sbuf", [128, PW], "float32"),
+    "l0": ("sbuf", [128, PW], "float32"),
+    "l1": ("sbuf", [128, PW], "float32"),
+    "l2": ("sbuf", [128, PW], "float32"),
+    "s": ("sbuf", [128, PW], "float32"),
+    "sq": ("sbuf", [128, PW], "float32"),
+    "q": ("sbuf", [128, 1], "float32"),
+    "qin": ("sbuf", [128, 2], "float32"),
     "ones": ("sbuf", [128, 128], "float32"),
     "geo": ("sbuf", [128, K], "float32"),
     "ntau": ("sbuf", [128, K], "float32"),
     "rt": ("sbuf", [128, K], "float32"),
     "env": ("sbuf", [128, K], "float32"),
     "col": ("sbuf", [128, 8], "float32"),
-    "acc": ("psum", [128, W], "float32"),
+    "acc": ("psum", [128, PW], "float32"),
     "tp": ("psum", [128, 1], "float32"),
 }
-SEMAPHORES = ["ld", "ldo", "sent", "r1", "a3", "ms", "tb", "ch", "yo", "st"]
+SEMAPHORES = ["ld", "ldo", "sh", "sent", "r1", "a3", "r3", "ms", "tb", "ch", "yo", "st"]
 
 
 def _peers(cores, topo, c):
@@ -50,6 +55,17 @@ def _peers(cores, topo, c):
 def _partner(cores, topo, c):
     return [x for x in cores if topo.rack(topo.host(x)) != topo.rack(topo.host(c)) and topo.may_write(c, x)
             and topo.chip(x) == topo.chip(c)][0]
+
+
+def _piece(cores, topo, c):
+    return tuple(sorted((cores.index(c), cores.index(_partner(cores, topo, c)))))
+
+
+def _runs(blocks):
+    x, y = blocks
+    if y == x + 1:
+        return [(x * F, 0, PW)]
+    return [(x * F, 0, F), (y * F, F, F)]
 
 
 def _count(mask):
@@ -62,7 +78,7 @@ def _halves(mask):
     return sum(bits[:h]), sum(bits[h:])
 
 
-def _hop1_masks(cores, topo, c):
+def _rack_masks(cores, topo, c):
     peers = _peers(cores, topo, c)
     return dict(zip(peers, _halves(topo.mask(c, peers[0]) & topo.mask(c, peers[1]))))
 
@@ -77,35 +93,62 @@ def rank_program(g, core, T, topo):
     Q, V, S, P = g.sync, g.vector, g.scalar, g.tensor
     peers = _peers(cores, topo, core)
     partner = _partner(cores, topo, core)
-    land = [T.l0, T.l1]
+    masks = _rack_masks(cores, topo, core)
+    landed = sum(_count(_rack_masks(cores, topo, p)[core]) for p in peers)
+    order = _piece(cores, topo, core)
+    piece = T.ownp[:]
 
-    Q.dma_start(T.gd[:], T.gr[:]).then_inc(sem.ld, 16)
-    Q.dma_start(T.own[:], T.gr[:]).then_inc(sem.ldo, 16)
+    queues = [Q, S]
+    nq = 0
+    for k, p in enumerate(peers):
+        for c0, d0, n in _runs(_piece(cores, topo, p)):
+            queues[nq % 2].dma_start(T.gd[k, :, d0:d0 + n], T.gr[:, c0:c0 + n]).then_inc(sem.ld, 16)
+            nq += 1
+    nld = 16 * nq
+    for c0, d0, n in _runs(order):
+        queues[nq % 2].dma_start(T.ownp[:, d0:d0 + n], T.gr[:, c0:c0 + n]).then_inc(sem.ldo, 16)
+        nq += 1
+    nldo = 16 * nq - nld
 
     sent = 0
     trs = []
-    masks = _hop1_masks(cores, topo, core)
-    for p in peers:
+    for k, p in enumerate(peers):
         rid, pid = topo.addr(p, core)
         trs.append(RemoteDMATransfer(dst_ids=[DstId(rid=rid, pnc=pid)], dma_engine_mask=masks[p], remote_sem=sem.r1,
-                                     src=T.gd[:], dst=land[_peers(cores, topo, p).index(core)][:]))
+                                     src=T.gd[k], dst=T.in1[_peers(cores, topo, p).index(core)]))
         sent += _count(masks[p])
-    g.wait_ge(sem.ld, 16)
+    g.wait_ge(sem.ld, nld)
     g.remote_dma_fused(trs, local_sem=sem.sent)
 
-    landed = sum(_count(_hop1_masks(cores, topo, p)[core]) for p in peers)
     m = topo.mask(core, partner)
     rid, pid = topo.addr(partner, core)
+    g.wait_ge(sem.ldo, nldo)
     g.wait_ge(sem.r1, landed)
     g.remote_dma_fused([RemoteDMATransfer(dst_ids=[DstId(rid=rid, pnc=pid)], dma_engine_mask=m, remote_sem=sem.a3,
-                                          srcs=[T.gd[:], T.l0[:], T.l1[:]], dsts=[T.l2[:]], alu_op=1)],
+                                          srcs=[piece, T.in1[0], T.in1[1]], dsts=[T.l2[:]], alu_op=1)],
                        local_sem=sem.sent)
     sent += _count(m)
 
+    Q.wait_ge(sem.r1, landed)
+    Q.dma_start(T.l0[:], T.in1[0]).then_inc(sem.sh, 16)
+    S.wait_ge(sem.r1, landed)
+    S.dma_start(T.l1[:], T.in1[1]).then_inc(sem.sh, 16)
+
+    trs = []
+    for p in peers:
+        rid, pid = topo.addr(p, core)
+        k = _peers(cores, topo, p).index(core)
+        trs.append(RemoteDMATransfer(dst_ids=[DstId(rid=rid, pnc=pid)], dma_engine_mask=masks[p], remote_sem=sem.r3,
+                                     src=T.q[:], dst=T.qin[:, k:k + 1]))
+        sent += _count(masks[p])
+    g.wait_ge(sem.ch, 4)
+    g.remote_dma_fused(trs, local_sem=sem.sent)
+
     col = T.col
-    q, t, a0, y1, a1, c = (col[:, i:i + 1] for i in range(6))
+    qs, t, a0, y1, a1, c = (col[:, i:i + 1] for i in range(6))
     y0 = T.env[:, K - 1:K]
-    mine = T.s[:, rank * F:(rank + 1) * F]
+    i0 = order.index(rank) * F
+    mine = T.s[:, i0:i0 + F]
 
     V.memset(T.ones[:], 1.0).then_inc(sem.ms, 1)
     V.memset(T.geo[:], 1.0 / RHO).then_inc(sem.ms, 1)
@@ -114,9 +157,9 @@ def rank_program(g, core, T, topo):
     V.wait_ge(sem.ms, 4)
     V.tensor_tensor_scan(T.ntau[:], T.geo[:], T.ones[:, 0:K], -RHO / TAU0, mult, mult).then_inc(sem.tb, 1)
 
-    V.wait_ge(sem.ldo, 16)
-    V.wait_ge(sem.r1, landed)
-    V.tensor_tensor(T.acc[:], T.own[:], T.l0[:], add).then_inc(sem.ch, 1)
+    V.wait_ge(sem.ldo, nldo)
+    V.wait_ge(sem.sh, 32)
+    V.tensor_tensor(T.acc[:], piece, T.l0[:], add).then_inc(sem.ch, 1)
     V.wait_ge(sem.ch, 1)
     V.tensor_tensor(T.acc[:], T.acc[:], T.l1[:], add).then_inc(sem.ch, 1)
     V.wait_ge(sem.a3, _count(topo.mask(partner, core)))
@@ -124,29 +167,33 @@ def rank_program(g, core, T, topo):
     V.tensor_tensor(T.s[:], T.acc[:], T.l2[:], add).then_inc(sem.ch, 1)
 
     S.wait_ge(sem.ch, 3)
-    S.activation(T.own[:], T.s[:], ActivationFunctionType.Square, scale=SIG / float(T.tables["BOUND"]),
-                 accum_out=q).then_inc(sem.ch, 1)
+    S.activation(T.sq[:], T.s[:], ActivationFunctionType.Square, scale=SIG / float(T.tables["BOUND"]),
+                 accum_out=T.q[:]).then_inc(sem.ch, 1)
+
+    V.wait_ge(sem.r3, landed)
+    V.wait_ge(sem.ch, 4)
+    V.tensor_scalar(qs, T.q[:], T.qin[:, 0:1], T.qin[:, 1:2], add, add).then_inc(sem.ch, 1)
     P.wait_ge(sem.ms, 4)
-    P.wait_ge(sem.ch, 4)
-    P.matmul(T.tp[:], T.ones[:], q, True, True).then_inc(sem.ch, 1)
+    P.wait_ge(sem.ch, 5)
+    P.matmul(T.tp[:], T.ones[:], qs, True, True).then_inc(sem.ch, 1)
 
     V.wait_ge(sem.tb, 1)
-    V.wait_ge(sem.ch, 5)
-    V.tensor_scalar(t, T.tp[:], TAU0, TAUL, amax, amin).then_inc(sem.ch, 1)
     V.wait_ge(sem.ch, 6)
-    V.tensor_scalar(T.geo[:], T.ntau[:], t, 3.0, mult, add).then_inc(sem.ch, 1)
+    V.tensor_scalar(t, T.tp[:], TAU0, TAUL, amax, amin).then_inc(sem.ch, 1)
     V.wait_ge(sem.ch, 7)
-    V.tensor_tensor_scan(T.env[:], T.geo[:], T.rt[:], -1.0e29, amax, mult).then_inc(sem.ch, 1)
+    V.tensor_scalar(T.geo[:], T.ntau[:], t, 3.0, mult, add).then_inc(sem.ch, 1)
     V.wait_ge(sem.ch, 8)
-    V.tensor_scalar(a0, y0, y0, t, mult, mult).then_inc(sem.ch, 1)
+    V.tensor_tensor_scan(T.env[:], T.geo[:], T.rt[:], -1.0e29, amax, mult).then_inc(sem.ch, 1)
     V.wait_ge(sem.ch, 9)
-    V.tensor_scalar(y1, a0, NEWTON1, y0, sub, mult).then_inc(sem.ch, 1)
+    V.tensor_scalar(a0, y0, y0, t, mult, mult).then_inc(sem.ch, 1)
     V.wait_ge(sem.ch, 10)
-    V.tensor_scalar(a1, y1, y1, t, mult, mult).then_inc(sem.ch, 1)
+    V.tensor_scalar(y1, a0, NEWTON1, y0, sub, mult).then_inc(sem.ch, 1)
     V.wait_ge(sem.ch, 11)
+    V.tensor_scalar(a1, y1, y1, t, mult, mult).then_inc(sem.ch, 1)
+    V.wait_ge(sem.ch, 12)
     V.tensor_scalar(c, a1, NEWTON2, y1, sub, mult).then_inc(sem.ch, 1)
 
-    V.wait_ge(sem.ch, 12)
+    V.wait_ge(sem.ch, 13)
     V.tensor_scalar(mine, mine, c, None, mult).then_inc(sem.yo, 1)
     Q.wait_ge(sem.yo, 1)
     Q.dma_start(T.y[:], mine).then_inc(sem.st, 16)

@@ -5,8 +5,8 @@ from concourse.mybir import AluOpType, ActivationFunctionType
 N, F = 6, 32
 W = N * F
 PW = 2 * F
-K = 128
-RHO = 2.0 ** 0.9
+K = 96
+RHO = 2.0 ** 1.2
 SIG = 2.0 ** -8
 TAU0 = SIG * SIG
 TAUL = TAU0 * RHO ** (K - 1)
@@ -34,7 +34,7 @@ SCRATCH = {
     "l2": ("sbuf", [128, PW], "float32"),
     "s": ("sbuf", [128, PW], "float32"),
     "sq": ("sbuf", [128, PW], "float32"),
-    "q": ("sbuf", [128, 1], "float32"),
+    "q": ("sbuf", [128, 2], "float32"),
     "qin": ("sbuf", [128, 2], "float32"),
     "ones": ("sbuf", [128, 128], "float32"),
     "geo": ("sbuf", [128, K], "float32"),
@@ -43,9 +43,9 @@ SCRATCH = {
     "env": ("sbuf", [128, K], "float32"),
     "col": ("sbuf", [128, 8], "float32"),
     "acc": ("psum", [128, PW], "float32"),
-    "tp": ("psum", [128, 1], "float32"),
+    "tp": ("psum", [128, 2], "float32"),
 }
-SEMAPHORES = ["ld", "ldo", "sh", "sent", "r1", "a3", "r3", "ms", "tb", "ch", "yo", "st"]
+SEMAPHORES = ["ld", "ldo", "sh0", "sh1", "sent", "r10", "r11", "a3", "r3", "ms", "tb", "ch", "sd", "yo", "st"]
 
 
 def _peers(cores, topo, c):
@@ -78,9 +78,13 @@ def _halves(mask):
     return sum(bits[:h]), sum(bits[h:])
 
 
-def _rack_masks(cores, topo, c):
+def _both(cores, topo, c):
     peers = _peers(cores, topo, c)
-    return dict(zip(peers, _halves(topo.mask(c, peers[0]) & topo.mask(c, peers[1]))))
+    return topo.mask(c, peers[0]) & topo.mask(c, peers[1])
+
+
+def _rack_masks(cores, topo, c):
+    return dict(zip(_peers(cores, topo, c), _halves(_both(cores, topo, c))))
 
 
 def rank_program(g, core, T, topo):
@@ -89,12 +93,13 @@ def rank_program(g, core, T, topo):
         return
     cores = list(T.cores)
     sem = T.sem
-    mult, add, amax, amin, sub = AluOpType.mult, AluOpType.add, AluOpType.max, AluOpType.min, AluOpType.subtract
+    mult, add, amax, sub = AluOpType.mult, AluOpType.add, AluOpType.max, AluOpType.subtract
     Q, V, S, P = g.sync, g.vector, g.scalar, g.tensor
     peers = _peers(cores, topo, core)
     partner = _partner(cores, topo, core)
     masks = _rack_masks(cores, topo, core)
-    landed = sum(_count(_rack_masks(cores, topo, p)[core]) for p in peers)
+    r1 = [sem.r10, sem.r11]
+    landed = [_count(_rack_masks(cores, topo, p)[core]) for p in peers]
     order = _piece(cores, topo, core)
     piece = T.ownp[:]
 
@@ -114,8 +119,9 @@ def rank_program(g, core, T, topo):
     trs = []
     for k, p in enumerate(peers):
         rid, pid = topo.addr(p, core)
-        trs.append(RemoteDMATransfer(dst_ids=[DstId(rid=rid, pnc=pid)], dma_engine_mask=masks[p], remote_sem=sem.r1,
-                                     src=T.gd[k], dst=T.in1[_peers(cores, topo, p).index(core)]))
+        slot = _peers(cores, topo, p).index(core)
+        trs.append(RemoteDMATransfer(dst_ids=[DstId(rid=rid, pnc=pid)], dma_engine_mask=masks[p], remote_sem=r1[slot],
+                                     src=T.gd[k], dst=T.in1[slot]))
         sent += _count(masks[p])
     g.wait_ge(sem.ld, nld)
     g.remote_dma_fused(trs, local_sem=sem.sent)
@@ -123,29 +129,33 @@ def rank_program(g, core, T, topo):
     m = topo.mask(core, partner)
     rid, pid = topo.addr(partner, core)
     g.wait_ge(sem.ldo, nldo)
-    g.wait_ge(sem.r1, landed)
+    g.wait_ge(r1[0], landed[0])
+    g.wait_ge(r1[1], landed[1])
     g.remote_dma_fused([RemoteDMATransfer(dst_ids=[DstId(rid=rid, pnc=pid)], dma_engine_mask=m, remote_sem=sem.a3,
                                           srcs=[piece, T.in1[0], T.in1[1]], dsts=[T.l2[:]], alu_op=1)],
                        local_sem=sem.sent)
     sent += _count(m)
 
-    Q.wait_ge(sem.r1, landed)
-    Q.dma_start(T.l0[:], T.in1[0]).then_inc(sem.sh, 16)
-    S.wait_ge(sem.r1, landed)
-    S.dma_start(T.l1[:], T.in1[1]).then_inc(sem.sh, 16)
+    Q.wait_ge(r1[0], landed[0])
+    Q.dma_start(T.l0[:], T.in1[0]).then_inc(sem.sh0, 16)
+    S.wait_ge(r1[1], landed[1])
+    S.dma_start(T.l1[:], T.in1[1]).then_inc(sem.sh1, 16)
 
-    trs = []
+    m3 = _both(cores, topo, core)
+    ids, dsts = [], []
     for p in peers:
         rid, pid = topo.addr(p, core)
         k = _peers(cores, topo, p).index(core)
-        trs.append(RemoteDMATransfer(dst_ids=[DstId(rid=rid, pnc=pid)], dma_engine_mask=masks[p], remote_sem=sem.r3,
-                                     src=T.q[:], dst=T.qin[:, k:k + 1]))
-        sent += _count(masks[p])
+        ids.append(DstId(rid=rid, pnc=pid))
+        dsts.append(T.qin[:, k:k + 1])
     g.wait_ge(sem.ch, 4)
-    g.remote_dma_fused(trs, local_sem=sem.sent)
+    g.remote_dma_fused([RemoteDMATransfer(dst_ids=ids, dma_engine_mask=m3, remote_sem=sem.r3, srcs=[T.q[:, 0:1]],
+                                          dsts=dsts, alu_op=0)], local_sem=sem.sent)
+    sent += _count(m3)
+    landed3 = sum(_count(_both(cores, topo, p)) for p in peers)
 
     col = T.col
-    qs, t, a0, y1, a1, c = (col[:, i:i + 1] for i in range(6))
+    t, a0, y1, d2, u = (col[:, i:i + 1] for i in range(5))
     y0 = T.env[:, K - 1:K]
     i0 = order.index(rank) * F
     mine = T.s[:, i0:i0 + F]
@@ -154,12 +164,14 @@ def rank_program(g, core, T, topo):
     V.memset(T.geo[:], 1.0 / RHO).then_inc(sem.ms, 1)
     V.memset(T.rt[:, 0:K - 1], math.sqrt(RHO)).then_inc(sem.ms, 1)
     V.memset(T.rt[:, K - 1:K], GLAST).then_inc(sem.ms, 1)
-    V.wait_ge(sem.ms, 4)
+    V.memset(T.q[:, 1:2], 0.0).then_inc(sem.ms, 1)
+    V.wait_ge(sem.ms, 5)
     V.tensor_tensor_scan(T.ntau[:], T.geo[:], T.ones[:, 0:K], -RHO / TAU0, mult, mult).then_inc(sem.tb, 1)
 
     V.wait_ge(sem.ldo, nldo)
-    V.wait_ge(sem.sh, 32)
+    V.wait_ge(sem.sh0, 16)
     V.tensor_tensor(T.acc[:], piece, T.l0[:], add).then_inc(sem.ch, 1)
+    V.wait_ge(sem.sh1, 16)
     V.wait_ge(sem.ch, 1)
     V.tensor_tensor(T.acc[:], T.acc[:], T.l1[:], add).then_inc(sem.ch, 1)
     V.wait_ge(sem.a3, _count(topo.mask(partner, core)))
@@ -168,33 +180,32 @@ def rank_program(g, core, T, topo):
 
     S.wait_ge(sem.ch, 3)
     S.activation(T.sq[:], T.s[:], ActivationFunctionType.Square, scale=SIG / float(T.tables["BOUND"]),
-                 accum_out=T.q[:]).then_inc(sem.ch, 1)
+                 accum_out=T.q[:, 0:1]).then_inc(sem.ch, 1)
 
-    V.wait_ge(sem.r3, landed)
-    V.wait_ge(sem.ch, 4)
-    V.tensor_scalar(qs, T.q[:], T.qin[:, 0:1], T.qin[:, 1:2], add, add).then_inc(sem.ch, 1)
-    P.wait_ge(sem.ms, 4)
-    P.wait_ge(sem.ch, 5)
-    P.matmul(T.tp[:], T.ones[:], qs, True, True).then_inc(sem.ch, 1)
+    P.wait_ge(sem.ms, 5)
+    P.wait_ge(sem.ch, 4)
+    P.matmul(T.tp[:], T.ones[:], T.q[:], True, False)
+    P.wait_ge(sem.r3, landed3)
+    P.matmul(T.tp[:], T.ones[:], T.qin[:], False, True).then_inc(sem.ch, 1)
 
     V.wait_ge(sem.tb, 1)
+    V.wait_ge(sem.ch, 5)
+    V.tensor_scalar(t, T.tp[:, 0:1], T.tp[:, 1:2], TAU0, add, amax).then_inc(sem.ch, 1)
     V.wait_ge(sem.ch, 6)
-    V.tensor_scalar(t, T.tp[:], TAU0, TAUL, amax, amin).then_inc(sem.ch, 1)
-    V.wait_ge(sem.ch, 7)
     V.tensor_scalar(T.geo[:], T.ntau[:], t, 3.0, mult, add).then_inc(sem.ch, 1)
-    V.wait_ge(sem.ch, 8)
+    V.wait_ge(sem.ch, 7)
     V.tensor_tensor_scan(T.env[:], T.geo[:], T.rt[:], -1.0e29, amax, mult).then_inc(sem.ch, 1)
-    V.wait_ge(sem.ch, 9)
+    V.wait_ge(sem.ch, 8)
     V.tensor_scalar(a0, y0, y0, t, mult, mult).then_inc(sem.ch, 1)
-    V.wait_ge(sem.ch, 10)
+    S.wait_ge(sem.ch, 9)
+    S.activation(d2, a0, ActivationFunctionType.Square, bias=-NEWTON1).then_inc(sem.sd, 1)
+    V.wait_ge(sem.ch, 9)
     V.tensor_scalar(y1, a0, NEWTON1, y0, sub, mult).then_inc(sem.ch, 1)
-    V.wait_ge(sem.ch, 11)
-    V.tensor_scalar(a1, y1, y1, t, mult, mult).then_inc(sem.ch, 1)
-    V.wait_ge(sem.ch, 12)
-    V.tensor_scalar(c, a1, NEWTON2, y1, sub, mult).then_inc(sem.ch, 1)
+    V.wait_ge(sem.sd, 1)
+    V.tensor_scalar(u, d2, a0, NEWTON2, mult, sub).then_inc(sem.ch, 1)
 
-    V.wait_ge(sem.ch, 13)
-    V.tensor_scalar(mine, mine, c, None, mult).then_inc(sem.yo, 1)
+    V.wait_ge(sem.ch, 11)
+    V.tensor_scalar(mine, mine, u, y1, mult, mult).then_inc(sem.yo, 1)
     Q.wait_ge(sem.yo, 1)
     Q.dma_start(T.y[:], mine).then_inc(sem.st, 16)
     Q.wait_ge(sem.st, 16)

import math
from concourse.bass import DstId, RemoteDMATransfer
from concourse.mybir import AluOpType, ActivationFunctionType

N, F = 6, 32
W = N * F
PW = 2 * F
K = 96
RHO = 2.0 ** 1.2
SIG = 2.0 ** -8
TAU0 = SIG * SIG
TAUL = TAU0 * RHO ** (K - 1)


def _dip():
    w = 1.0
    for i in range(2001):
        e = 1.0 + (RHO - 1.0) * i / 2000.0
        w = min(w, max(1.5 - 0.5 * e, (1.5 - 0.5 * e / RHO) / math.sqrt(RHO)) * math.sqrt(e))
    return 1.0 - w


LAM = (SIG / 16.0) ** (1.0 / 9.0)
GLAST = 0.5 * LAM / (1.0 - 0.5 * _dip()) / math.sqrt(TAUL)
NEWTON1 = 3.0 * LAM ** 2
NEWTON2 = 12.0 * LAM ** 6

SCRATCH = {
    "gd": ("dram", [2, 128, PW], "float32"),
    "in1": ("dram", [2, 128, PW], "float32"),
    "ownp": ("sbuf", [128, PW], "float32"),
    "l0": ("sbuf", [128, PW], "float32"),
    "l1": ("sbuf", [128, PW], "float32"),
    "l2": ("sbuf", [128, PW], "float32"),
    "s": ("sbuf", [128, PW], "float32"),
    "sq": ("sbuf", [128, PW], "float32"),
    "q": ("sbuf", [128, 2], "float32"),
    "qin": ("sbuf", [128, 2], "float32"),
    "ones": ("sbuf", [128, 128], "float32"),
    "geo": ("sbuf", [128, K], "float32"),
    "ntau": ("sbuf", [128, K], "float32"),
    "rt": ("sbuf", [128, K], "float32"),
    "env": ("sbuf", [128, K], "float32"),
    "col": ("sbuf", [128, 8], "float32"),
    "acc": ("psum", [128, PW], "float32"),
    "tp": ("psum", [128, 2], "float32"),
}
SEMAPHORES = ["ld", "ldo", "sh0", "sh1", "sent", "r10", "r11", "a3", "r3", "ms", "tb", "ch", "sd", "yo", "st"]


def _peers(cores, topo, c):
    return [x for x in cores if x != c and topo.rack(topo.host(x)) == topo.rack(topo.host(c))]


def _partner(cores, topo, c):
    return [x for x in cores if topo.rack(topo.host(x)) != topo.rack(topo.host(c)) and topo.may_write(c, x)
            and topo.chip(x) == topo.chip(c)][0]


def _piece(cores, topo, c):
    return tuple(sorted((cores.index(c), cores.index(_partner(cores, topo, c)))))


def _runs(blocks):
    x, y = blocks
    if y == x + 1:
        return [(x * F, 0, PW)]
    return [(x * F, 0, F), (y * F, F, F)]


def _count(mask):
    return bin(mask).count("1")


def _halves(mask):
    bits = [1 << i for i in range(mask.bit_length()) if (mask >> i) & 1]
    h = len(bits) // 2
    return sum(bits[:h]), sum(bits[h:])


def _both(cores, topo, c):
    peers = _peers(cores, topo, c)
    return topo.mask(c, peers[0]) & topo.mask(c, peers[1])


def _rack_masks(cores, topo, c):
    return dict(zip(_peers(cores, topo, c), _halves(_both(cores, topo, c))))


def rank_program(g, core, T, topo):
    rank = T.rank_of(core)
    if rank is None:
        return
    cores = list(T.cores)
    sem = T.sem
    mult, add, amax, sub = AluOpType.mult, AluOpType.add, AluOpType.max, AluOpType.subtract
    Q, V, S, P = g.sync, g.vector, g.scalar, g.tensor
    peers = _peers(cores, topo, core)
    partner = _partner(cores, topo, core)
    masks = _rack_masks(cores, topo, core)
    r1 = [sem.r10, sem.r11]
    landed = [_count(_rack_masks(cores, topo, p)[core]) for p in peers]
    order = _piece(cores, topo, core)
    piece = T.ownp[:]

    queues = [Q, S]
    nq = 0
    for k, p in enumerate(peers):
        for c0, d0, n in _runs(_piece(cores, topo, p)):
            queues[nq % 2].dma_start(T.gd[k, :, d0:d0 + n], T.gr[:, c0:c0 + n]).then_inc(sem.ld, 16)
            nq += 1
    nld = 16 * nq
    for c0, d0, n in _runs(order):
        queues[nq % 2].dma_start(T.ownp[:, d0:d0 + n], T.gr[:, c0:c0 + n]).then_inc(sem.ldo, 16)
        nq += 1
    nldo = 16 * nq - nld

    sent = 0
    trs = []
    for k, p in enumerate(peers):
        rid, pid = topo.addr(p, core)
        slot = _peers(cores, topo, p).index(core)
        trs.append(RemoteDMATransfer(dst_ids=[DstId(rid=rid, pnc=pid)], dma_engine_mask=masks[p], remote_sem=r1[slot],
                                     src=T.gd[k], dst=T.in1[slot]))
        sent += _count(masks[p])
    g.wait_ge(sem.ld, nld)
    g.remote_dma_fused(trs, local_sem=sem.sent)

    m = topo.mask(core, partner)
    rid, pid = topo.addr(partner, core)
    g.wait_ge(sem.ldo, nldo)
    g.wait_ge(r1[0], landed[0])
    g.wait_ge(r1[1], landed[1])
    g.remote_dma_fused([RemoteDMATransfer(dst_ids=[DstId(rid=rid, pnc=pid)], dma_engine_mask=m, remote_sem=sem.a3,
                                          srcs=[piece, T.in1[0], T.in1[1]], dsts=[T.l2[:]], alu_op=1)],
                       local_sem=sem.sent)
    sent += _count(m)

    Q.wait_ge(r1[0], landed[0])
    Q.dma_start(T.l0[:], T.in1[0]).then_inc(sem.sh0, 16)
    S.wait_ge(r1[1], landed[1])
    S.dma_start(T.l1[:], T.in1[1]).then_inc(sem.sh1, 16)

    m3 = _both(cores, topo, core)
    ids, dsts = [], []
    for p in peers:
        rid, pid = topo.addr(p, core)
        k = _peers(cores, topo, p).index(core)
        ids.append(DstId(rid=rid, pnc=pid))
        dsts.append(T.qin[:, k:k + 1])
    g.wait_ge(sem.ch, 4)
    g.remote_dma_fused([RemoteDMATransfer(dst_ids=ids, dma_engine_mask=m3, remote_sem=sem.r3, srcs=[T.q[:, 0:1]],
                                          dsts=dsts, alu_op=0)], local_sem=sem.sent)
    sent += _count(m3)
    landed3 = sum(_count(_both(cores, topo, p)) for p in peers)

    col = T.col
    t, a0, y1, d2, u = (col[:, i:i + 1] for i in range(5))
    y0 = T.env[:, K - 1:K]
    i0 = order.index(rank) * F
    mine = T.s[:, i0:i0 + F]

    V.memset(T.ones[:], 1.0).then_inc(sem.ms, 1)
    V.memset(T.geo[:], 1.0 / RHO).then_inc(sem.ms, 1)
    V.memset(T.rt[:, 0:K - 1], math.sqrt(RHO)).then_inc(sem.ms, 1)
    V.memset(T.rt[:, K - 1:K], GLAST).then_inc(sem.ms, 1)
    V.memset(T.q[:, 1:2], 0.0).then_inc(sem.ms, 1)
    V.wait_ge(sem.ms, 5)
    V.tensor_tensor_scan(T.ntau[:], T.geo[:], T.ones[:, 0:K], -RHO / TAU0, mult, mult).then_inc(sem.tb, 1)

    V.wait_ge(sem.ldo, nldo)
    V.wait_ge(sem.sh0, 16)
    V.tensor_tensor(T.acc[:], piece, T.l0[:], add).then_inc(sem.ch, 1)
    V.wait_ge(sem.sh1, 16)
    V.wait_ge(sem.ch, 1)
    V.tensor_tensor(T.acc[:], T.acc[:], T.l1[:], add).then_inc(sem.ch, 1)
    V.wait_ge(sem.a3, _count(topo.mask(partner, core)))
    V.wait_ge(sem.ch, 2)
    V.tensor_tensor(T.s[:], T.acc[:], T.l2[:], add).then_inc(sem.ch, 1)

    S.wait_ge(sem.ch, 3)
    S.activation(T.sq[:], T.s[:], ActivationFunctionType.Square, scale=SIG / float(T.tables["BOUND"]),
                 accum_out=T.q[:, 0:1]).then_inc(sem.ch, 1)

    P.wait_ge(sem.ms, 5)
    P.wait_ge(sem.ch, 4)
    P.matmul(T.tp[:], T.ones[:], T.q[:], True, False)
    P.wait_ge(sem.r3, landed3)
    P.matmul(T.tp[:], T.ones[:], T.qin[:], False, True).then_inc(sem.ch, 1)

    V.wait_ge(sem.tb, 1)
    V.wait_ge(sem.ch, 5)
    V.tensor_scalar(t, T.tp[:, 0:1], T.tp[:, 1:2], TAU0, add, amax).then_inc(sem.ch, 1)
    V.wait_ge(sem.ch, 6)
    V.tensor_scalar(T.geo[:], T.ntau[:], t, 3.0, mult, add).then_inc(sem.ch, 1)
    V.wait_ge(sem.ch, 7)
    V.tensor_tensor_scan(T.env[:], T.geo[:], T.rt[:], -1.0e29, amax, mult).then_inc(sem.ch, 1)
    V.wait_ge(sem.ch, 8)
    V.tensor_scalar(a0, y0, y0, t, mult, mult).then_inc(sem.ch, 1)
    S.wait_ge(sem.ch, 9)
    S.activation(d2, a0, ActivationFunctionType.Square, bias=-NEWTON1).then_inc(sem.sd, 1)
    V.wait_ge(sem.ch, 9)
    V.tensor_scalar(y1, a0, NEWTON1, y0, sub, mult).then_inc(sem.ch, 1)
    V.wait_ge(sem.sd, 1)
    V.tensor_scalar(u, d2, a0, NEWTON2, mult, sub).then_inc(sem.ch, 1)

    V.wait_ge(sem.ch, 11)
    V.tensor_scalar(mine, mine, u, y1, mult, mult).then_inc(sem.yo, 1)
    Q.wait_ge(sem.yo, 1)
    Q.dma_start(T.y[:], mine).then_inc(sem.st, 16)
    Q.wait_ge(sem.st, 16)
    g.wait_ge(sem.sent, sent)
